import numpy as np
import ml_dtypes


def mxq(x, axis, fmt="e4m3"):
    dtype, down = {"e4m3": (ml_dtypes.float8_e4m3fn, 7), "e5m2": (ml_dtypes.float8_e5m2, 14)}[fmt]
    v = np.moveaxis(np.asarray(x, np.float32).astype(ml_dtypes.bfloat16).astype(np.float64), axis, -1)
    blocks = v.reshape(v.shape[:-1] + (-1, 32))
    amax = np.abs(blocks).max(-1, keepdims=True)
    byte = np.maximum(np.where(amax > 0, np.frexp(amax)[1] - 1 + 127, 0) - down, 1)
    scale = np.exp2(byte - 127.0)
    codes = (blocks / scale).astype(np.float32).astype(dtype).astype(np.float64)
    return np.moveaxis((codes * scale).reshape(v.shape), -1, axis)


WIDE = False


def mx_kscale(k):
    if not WIDE:
        return np.ones(k)
    levels = np.array([10, -10, 5, -5, 0])
    if k % 512:
        return np.exp2(np.random.permutation(np.resize(levels, k // 32))).repeat(32)
    a = np.empty((k // 512, 16))
    for p in range(k // 512):
        a[p, :8] = np.random.permutation(np.resize(levels, 8))
        for g in range(8):
            far = levels[np.abs(levels - a[p, g]) >= 10]
            a[p, g + 8] = far[np.random.randint(len(far))]
    return np.exp2(a.ravel()).repeat(32)


def f64(x):
    return np.asarray(x).astype(np.float64)


def striped8(idx):
    return np.asarray(idx).reshape(8, -1, 16).transpose(0, 2, 1).reshape(128, -1).astype(np.uint16)


def unstriped8(offs):
    return offs.reshape(8, 16, -1).transpose(0, 2, 1).reshape(8, -1).astype(np.int64)


def pick8(x, idx, run):
    r = np.arange(len(x))
    return x[r[:, None], idx[r % (8 * run) // run]]


E2M1 = np.array([0.0, 0.5, 1.0, 1.5, 2.0, 3.0, 4.0, 6.0, -0.0, -0.5, -1.0, -1.5, -2.0, -3.0, -4.0, -6.0])


def pack_weight(w, fmt):
    k, n = w.shape
    w = f64(np.asarray(w, np.float32).astype(ml_dtypes.bfloat16)).reshape(k // 32, 32, n)
    amax = np.abs(w).max(1)
    if fmt == "e4m3":
        byte = np.frexp(amax)[1] - 1 + 127 - 7
    else:
        mant, ex = np.frexp(amax / 6.0)
        byte = np.where(mant > 0.5, ex, ex - 1) + 127
    byte = np.clip(np.where(amax > 0, byte, 1), 1, 254)
    scaled = (w * np.exp2(127.0 - byte)[:, None, :]).reshape(k, n).astype(np.float32)
    by_word = np.ascontiguousarray(scaled.reshape(k // 512, 128, 4, n).transpose(0, 1, 3, 2))
    if fmt == "e4m3":
        words = by_word.astype(ml_dtypes.float8_e4m3fn).view(np.uint8)
    else:
        c = by_word.astype(ml_dtypes.float4_e2m1fn).view(np.uint8) & 0xF
        words = (c[..., 0::2] | (c[..., 1::2] << 4)).reshape(k // 512, 128, 2 * n)
    return np.ascontiguousarray(words), np.ascontiguousarray(byte.astype(np.uint8).reshape(k // 512, 16, n))


def unpack_weight(words, scales, fmt):
    g, _, n = scales.shape
    words = np.ascontiguousarray(words).reshape(g, 128, n, -1)
    if fmt == "e4m3":
        vals = words.view(ml_dtypes.float8_e4m3fn).astype(np.float64)
    else:
        nib = np.empty((g, 128, n, 4), np.uint8)
        nib[..., 0::2] = words & 0xF
        nib[..., 1::2] = words >> 4
        vals = E2M1[nib]
    vals = vals * np.repeat(np.exp2(scales.astype(np.float64) - 127.0), 8, axis=1)[..., None]
    return vals.transpose(0, 1, 3, 2).reshape(g * 512, n)


D, T, I, Q = 512, 1024, 512, 128


def setup_inputs():
    n = np.random.standard_normal
    idx = np.stack([np.random.permutation(T)[:I] for _ in range(8)])
    idx2 = np.stack([np.random.permutation(T)[:I] for _ in range(8)])
    fd = mx_kscale(D)
    keysp = pack_weight(n((D, T)) / fd[:, None], "e2m1")
    return {
        "query": (n((D, Q)) * 1.0 / np.sqrt(D) * fd[:, None]).astype(np.float32),
        "query2": (n((D, Q)) * 1.0 / np.sqrt(D) * fd[:, None]).astype(np.float32),
        "keys_words": keysp[0],
        "keys_scales": keysp[1],
        "lam": (np.random.uniform(1.0, 3.0, (Q, 1))).astype(np.float32),
        "smear": (np.random.uniform(0.3, 0.8, (Q, 1))).astype(np.float32),
        "old": (np.random.uniform(0.0, 2.0, (Q, T))).astype(np.float32),
        "fade": (np.random.uniform(0.3, 0.9, (Q, 1))).astype(np.float32),
        "offs": striped8(idx),
        "offs2": striped8(idx2),
    }


def reference(query, query2, keys_words, keys_scales, lam, smear, old, fade, offs, offs2):
    idx = unstriped8(offs)
    idx2 = unstriped8(offs2)
    keysu = unpack_weight(keys_words, keys_scales, "e2m1")
    queryq = mxq(f64(query), 0, "e4m3")
    a = queryq.T @ keysu
    query2q = mxq(f64(query2), 0, "e4m3")
    b = query2q.T @ keysu
    la = np.square(pick8(a, idx, 16)) + np.square(pick8(b, idx, 16))
    lb = np.square(pick8(a, idx2, 16)) + np.square(pick8(b, idx2, 16))
    s = (pick8(a, idx, 16) * pick8(a, idx2, 16) + pick8(b, idx, 16) * pick8(b, idx2, 16)) / np.sqrt(la * lb + 0.5) * f64(lam)
    p = np.exp(s - np.max(s, axis=1, keepdims=True))
    r = p / np.sum(p, axis=1, keepdims=True)
    r1 = np.pad(r, ((0, 0), (1, 0)))[:, :I]
    r2 = np.pad(r, ((0, 0), (2, 0)))[:, :I]
    w = r + r1 * f64(smear) + r2 * np.square(f64(smear))
    ws = w * 256.0
    wf = np.zeros((Q, T))
    wf[np.arange(Q)[:, None], idx[np.arange(Q) % 128 // 16]] = ws
    y = f64(old) * f64(fade) + wf
    return y

@@ -1,0 +1,155 @@
+from contextlib import ExitStack
+
+import concourse.mybir as mybir
+
+D, T, I, Q = 512, 1024, 512, 128
+FLOPS = 2 * 2 * D * T * Q
+
+F32 = mybir.dt.float32
+BF16 = mybir.dt.bfloat16
+I32 = mybir.dt.int32
+U32 = mybir.dt.uint32
+U16 = mybir.dt.uint16
+U8 = mybir.dt.uint8
+FP8X4 = mybir.dt.float8_e4m3fn_x4
+FP4X4 = mybir.dt.float4_e2m1fn_x4
+ALU = mybir.AluOpType
+ACT = mybir.ActivationFunctionType
+
+P = 128
+PACK = 4
+BANK = 256
+PAD = 8
+
+
+def tile_attend_planecos_smeared_counts_heads_kernel(
+    tc, query, query2, keys_words, keys_scales, lam, smear, old, fade, offs, offs2, out
+):
+    nc = tc.nc
+    with ExitStack() as ctx:
+        sb = ctx.enter_context(tc.tile_pool(name="sb", bufs=1))
+        psum = ctx.enter_context(tc.psum_pool(name="psum", bufs=1))
+
+        list1 = sb.tile([P, I // 16], U16, name="list1")
+        list2 = sb.tile([P, I // 16], U16, name="list2")
+        raw = [sb.tile([P, PACK, Q], F32, name=f"raw{j}") for j in range(2)]
+        words = sb.tile([P, 2 * T], U8, name="words", align_bytes=64)
+        kscale = sb.tile([P, T], U8, name="kscale", align_bytes=64)
+        lam_c = sb.tile([P, 1], F32, name="lam_c")
+        smear_c = sb.tile([P, 1], F32, name="smear_c")
+        fade_c = sb.tile([P, 1], F32, name="fade_c")
+        old_t = sb.tile([P, T], F32, name="old_t")
+        placed = sb.tile([P, T], F32, name="placed")
+        half = sb.tile([P, 1], F32, name="half")
+        p = sb.tile([P, PAD + I], F32, name="p")
+        t = sb.tile([P, PAD + I], F32, name="t")
+
+        nc.sync.dma_start(out=raw[0][:], in_=query.rearrange("(p j) q -> p j q", j=PACK))
+        nc.sync.dma_start(out=words[:].bitcast(I32), in_=keys_words[0].bitcast(I32))
+        for quad in range(4):
+            nc.scalar.dma_start(
+                out=kscale[32 * quad : 32 * quad + 4, :].bitcast(I32),
+                in_=keys_scales[0, 4 * quad : 4 * quad + 4, :].bitcast(I32),
+            )
+        nc.sync.dma_start(out=raw[1][:], in_=query2.rearrange("(p j) q -> p j q", j=PACK))
+        nc.sync.dma_start(list1[:], offs)
+        nc.sync.dma_start(list2[:], offs2)
+        nc.sync.dma_start(out=smear_c[:], in_=smear)
+        nc.sync.dma_start(out=lam_c[:], in_=lam)
+        nc.sync.dma_start(out=fade_c[:], in_=fade)
+        nc.sync.dma_start(out=old_t[:], in_=old)
+        nc.vector.memset(half[:], 0.5)
+        nc.vector.memset(placed[:], 0.0)
+        nc.vector.memset(p[:, 0:PAD], 0.0)
+        nc.vector.memset(t[:, 0:PAD], 0.0)
+
+        planes = []
+        for j in range(2):
+            grouped = sb.tile([P, Q, PACK], BF16, name=f"grouped{j}", align_bytes=64)
+            codes = sb.tile([P, Q], U32, name=f"codes{j}", align_bytes=64)
+            qscale = sb.tile([P, Q], U8, name=f"qscale{j}", align_bytes=64)
+            nc.vector.tensor_copy(out=grouped[:], in_=raw[j][:].rearrange("p j q -> p q j"))
+            nc.vector.quantize_mx(
+                out=codes[:].bitcast(FP8X4), scales=qscale[:], in_=grouped[:].rearrange("p q j -> p (q j)")
+            )
+            plane = sb.tile([P, T], F32, name=f"plane{j}", tag=f"plane{j}")
+            for h in range(T // BANK):
+                acc = psum.tile([P, BANK], F32, name=f"acc{j}{h}")
+                nc.tensor.matmul_mx(
+                    out=acc[:],
+                    lhsT=codes[:].bitcast(FP8X4),
+                    lhsT_scale=qscale[:],
+                    rhs=words[:, 2 * BANK * h : 2 * BANK * (h + 1)].bitcast(FP4X4),
+                    rhs_scale=kscale[:, BANK * h : BANK * (h + 1)],
+                    start=True,
+                    stop=True,
+                )
+                cols = plane[:, BANK * h : BANK * (h + 1)]
+                if j == 0 and h % 2 == 1:
+                    nc.vector.tensor_copy(out=cols, in_=acc[:])
+                else:
+                    nc.scalar.copy(out=cols, in_=acc[:])
+            planes.append(plane)
+        a, b = planes
+
+        def work(name):
+            return sb.tile([P, I], F32, name=name)
+
+        H = I // 2
+        halves = [slice(0, H), slice(H, I)]
+        g1 = sb.tile([P, 2 * I], F32, name="g1")
+        g2 = sb.tile([P, 2 * I], F32, name="g2")
+        m = sb.tile([P, 2 * I], F32, name="m")
+        a1, b1, a2, b2 = g1[:, 0:I], g1[:, I : 2 * I], g2[:, 0:I], g2[:, I : 2 * I]
+        sa1, sb1, sb2 = work("sa1"), work("sb1"), work("sb2")
+        lb, den, rs, s = work("lb"), work("den"), work("rs"), work("s")
+        nc.vector.tensor_copy(a1, a[:].indirect(list1[:]))
+        nc.vector.tensor_copy(a2, a[:].indirect(list2[:]))
+        nc.scalar.activation(b1, b[:].indirect(list1[:]), ACT.Copy)
+        nc.scalar.activation(b2, b[:].indirect(list2[:]), ACT.Copy)
+        nc.scalar.activation(sb1[:], b1, ACT.Square)
+        for h in halves:
+            nc.scalar.activation(sb2[:, h], b2[:, h], ACT.Square)
+        sa2 = [sb.tile([P, H], F32, name="sa2_lo"), sb.tile([P, H], F32, name="sa2_hi", tag="plane1")]
+        nc.scalar.activation(sa2[1][:], a2[:, halves[1]], ACT.Square)
+        nc.vector.tensor_tensor(sa1[:], a1, a1, ALU.mult)
+        nc.vector.tensor_tensor(sa2[0][:], a2[:, halves[0]], a2[:, halves[0]], ALU.mult)
+        nc.vector.tensor_tensor(m[:, 0:I], a1, a2, ALU.mult)
+        nc.vector.tensor_tensor(m[:, I : 2 * I], b1, b2, ALU.mult)
+        la = b1
+        nc.vector.tensor_tensor(la, sa1[:], sb1[:], ALU.add)
+        for j, h in enumerate(halves):
+            nc.vector.tensor_tensor(lb[:, h], sa2[j][:], sb2[:, h], ALU.add)
+        for h in halves:
+            nc.vector.tensor_tensor(den[:, h], la[:, h], lb[:, h], ALU.mult)
+            nc.scalar.activation(rs[:, h], den[:, h], ACT.Abs_reciprocal_sqrt, bias=half[:])
+        dot = sb2
+        nc.vector.tensor_tensor(dot[:], m[:, 0:I], m[:, I : 2 * I], ALU.add)
+        for h in halves:
+            nc.vector.scalar_tensor_tensor(s[:, h], dot[:, h], lam_c[:], rs[:, h], ALU.mult, ALU.mult)
+        negmax = sb.tile([P, 1], F32, name="negmax")
+        nc.vector.tensor_reduce(negmax[:], s[:], mybir.AxisListType.X, ALU.max, negate=True)
+
+        total = sb.tile([P, 1], F32, name="total")
+        inv = sb.tile([P, 1], F32, name="inv")
+        gain = sb.tile([P, 1], F32, name="gain")
+        own, behind = work("own"), work("behind")
+        nc.scalar.activation(p[:, PAD : PAD + I], s[:], ACT.Exp, bias=negmax[:], accum_out=total[:])
+        nc.vector.reciprocal(inv[:], total[:])
+        for h in halves:
+            lo, hi = PAD + h.start, PAD + h.stop
+            nc.vector.scalar_tensor_tensor(t[:, lo:hi], p[:, lo - 1 : hi - 1], smear_c[:], p[:, lo:hi], ALU.mult, ALU.add)
+            if h.start == 0:
+                nc.vector.tensor_scalar(gain[:], inv[:], 256.0, None, ALU.mult)
+        nc.scalar.activation(own[:], p[:, PAD : PAD + I], ACT.Copy, scale=gain[:])
+        for h in halves:
+            lo, hi = PAD + h.start, PAD + h.stop
+            nc.vector.tensor_scalar(behind[:, h], t[:, lo - 1 : hi - 1], gain[:], smear_c[:], ALU.mult, ALU.mult)
+        nc.vector.tensor_tensor(placed[:].indirect(list1[:]), own[:], behind[:], ALU.add)
+
+        res = sb.tile([P, T], F32, name="res")
+        step = T // 4
+        for c in range(4):
+            cols = slice(c * step, (c + 1) * step)
+            nc.vector.scalar_tensor_tensor(res[:, cols], old_t[:, cols], fade_c[:], placed[:, cols], ALU.mult, ALU.add)
+            (nc.sync if c % 2 == 0 else nc.scalar).dma_start(out=out[:, cols], in_=res[:, cols])

@@ -59,6 +59,8 @@ def tile_attend_planecos_smeared_counts_heads_kernel(
         nc.sync.dma_start(out=fade_c[:], in_=fade)
         nc.sync.dma_start(out=old_t[:], in_=old)
         nc.vector.memset(half[:], 0.5)
+        warm = sb.tile([P, 1], F32, name="warm")
+        nc.scalar.activation(warm[:], half[:], ACT.Abs_reciprocal_sqrt, bias=half[:])
         nc.vector.memset(placed[:], 0.0)
         nc.vector.memset(p[:, 0:PAD], 0.0)
         nc.vector.memset(t[:, 0:PAD], 0.0)

@@ -18,7 +18,7 @@ ACT = mybir.ActivationFunctionType
 
 P = 128
 PACK = 4
-BANK = 256
+EDGES = [0, 256, 512, 768, 896, 1024]
 PAD = 8
 
 
@@ -75,18 +75,20 @@ def tile_attend_planecos_smeared_counts_heads_kernel(
                 out=codes[:].bitcast(FP8X4), scales=qscale[:], in_=grouped[:].rearrange("p q j -> p (q j)")
             )
             plane = sb.tile([P, T], F32, name=f"plane{j}", tag=f"plane{j}")
-            for h in range(T // BANK):
-                acc = psum.tile([P, BANK], F32, name=f"acc{j}{h}")
+            for h in range(len(EDGES) - 1):
+                lo, hi = EDGES[h], EDGES[h + 1]
+                bank = (j * (len(EDGES) - 1) + h) % 8
+                acc = psum.tile([P, hi - lo], F32, name=f"acc{j}{h}", tag=f"acc0{bank}")
                 nc.tensor.matmul_mx(
                     out=acc[:],
                     lhsT=codes[:].bitcast(FP8X4),
                     lhsT_scale=qscale[:],
-                    rhs=words[:, 2 * BANK * h : 2 * BANK * (h + 1)].bitcast(FP4X4),
-                    rhs_scale=kscale[:, BANK * h : BANK * (h + 1)],
+                    rhs=words[:, 2 * lo : 2 * hi].bitcast(FP4X4),
+                    rhs_scale=kscale[:, lo:hi],
                     start=True,
                     stop=True,
                 )
-                cols = plane[:, BANK * h : BANK * (h + 1)]
+                cols = plane[:, lo:hi]
                 if j == 0 and h % 2 == 1:
                     nc.vector.tensor_copy(out=cols, in_=acc[:])
                 else:
@@ -104,7 +106,7 @@ def tile_attend_planecos_smeared_counts_heads_kernel(
         m = sb.tile([P, 2 * I], F32, name="m")
         a1, b1, a2, b2 = g1[:, 0:I], g1[:, I : 2 * I], g2[:, 0:I], g2[:, I : 2 * I]
         sa1, sb1, sb2 = work("sa1"), work("sb1"), work("sb2")
-        lb, den, rs, s = work("lb"), work("den"), work("rs"), work("s")
+        den, rs, s = work("den"), work("rs"), work("s")
         nc.vector.tensor_copy(a1, a[:].indirect(list1[:]))
         nc.vector.tensor_copy(a2, a[:].indirect(list2[:]))
         nc.scalar.activation(b1, b[:].indirect(list1[:]), ACT.Copy)
@@ -112,21 +114,23 @@ def tile_attend_planecos_smeared_counts_heads_kernel(
         nc.scalar.activation(sb1[:], b1, ACT.Square)
         for h in halves:
             nc.scalar.activation(sb2[:, h], b2[:, h], ACT.Square)
-        sa2 = [sb.tile([P, H], F32, name="sa2_lo"), sb.tile([P, H], F32, name="sa2_hi", tag="plane1")]
-        nc.scalar.activation(sa2[1][:], a2[:, halves[1]], ACT.Square)
-        nc.vector.tensor_tensor(sa1[:], a1, a1, ALU.mult)
-        nc.vector.tensor_tensor(sa2[0][:], a2[:, halves[0]], a2[:, halves[0]], ALU.mult)
+        sa2 = work("sa2")
+        nc.gpsimd.tensor_tensor(sa1[:], a1, a1, ALU.mult)
+        nc.vector.tensor_tensor(sa2[:], a2, a2, ALU.mult)
         nc.vector.tensor_tensor(m[:, 0:I], a1, a2, ALU.mult)
         nc.vector.tensor_tensor(m[:, I : 2 * I], b1, b2, ALU.mult)
-        la = b1
-        nc.vector.tensor_tensor(la, sa1[:], sb1[:], ALU.add)
+        la = work("la")
+        for h in halves:
+            nc.vector.tensor_tensor(la[:, h], sa1[:, h], sb1[:, h], ALU.add)
+        lb = sb1
         for j, h in enumerate(halves):
-            nc.vector.tensor_tensor(lb[:, h], sa2[j][:], sb2[:, h], ALU.add)
+            nc.vector.tensor_tensor(lb[:, h], sa2[:, h], sb2[:, h], ALU.add)
         for h in halves:
             nc.vector.tensor_tensor(den[:, h], la[:, h], lb[:, h], ALU.mult)
             nc.scalar.activation(rs[:, h], den[:, h], ACT.Abs_reciprocal_sqrt, bias=half[:])
-        dot = sb2
-        nc.vector.tensor_tensor(dot[:], m[:, 0:I], m[:, I : 2 * I], ALU.add)
+        dot = lb
+        for h in halves:
+            nc.vector.tensor_tensor(dot[:, h], m[:, h], m[:, I + h.start : I + h.stop], ALU.add)
         for h in halves:
             nc.vector.scalar_tensor_tensor(s[:, h], dot[:, h], lam_c[:], rs[:, h], ALU.mult, ALU.mult)
         negmax = sb.tile([P, 1], F32, name="negmax")

from contextlib import ExitStack

import concourse.mybir as mybir

D, T, I, Q = 512, 1024, 512, 128
FLOPS = 2 * 2 * D * T * Q

F32 = mybir.dt.float32
BF16 = mybir.dt.bfloat16
I32 = mybir.dt.int32
U32 = mybir.dt.uint32
U16 = mybir.dt.uint16
U8 = mybir.dt.uint8
FP8X4 = mybir.dt.float8_e4m3fn_x4
FP4X4 = mybir.dt.float4_e2m1fn_x4
ALU = mybir.AluOpType
ACT = mybir.ActivationFunctionType

P = 128
PACK = 4
EDGES = [0, 256, 512, 768, 896, 1024]
PAD = 8


def tile_attend_planecos_smeared_counts_heads_kernel(
    tc, query, query2, keys_words, keys_scales, lam, smear, old, fade, offs, offs2, out
):
    nc = tc.nc
    with ExitStack() as ctx:
        sb = ctx.enter_context(tc.tile_pool(name="sb", bufs=1))
        psum = ctx.enter_context(tc.psum_pool(name="psum", bufs=1))

        list1 = sb.tile([P, I // 16], U16, name="list1")
        list2 = sb.tile([P, I // 16], U16, name="list2")
        raw = [sb.tile([P, PACK, Q], F32, name=f"raw{j}") for j in range(2)]
        words = sb.tile([P, 2 * T], U8, name="words", align_bytes=64)
        kscale = sb.tile([P, T], U8, name="kscale", align_bytes=64)
        lam_c = sb.tile([P, 1], F32, name="lam_c")
        smear_c = sb.tile([P, 1], F32, name="smear_c")
        fade_c = sb.tile([P, 1], F32, name="fade_c")
        old_t = sb.tile([P, T], F32, name="old_t")
        placed = sb.tile([P, T], F32, name="placed")
        half = sb.tile([P, 1], F32, name="half")
        p = sb.tile([P, PAD + I], F32, name="p")
        t = sb.tile([P, PAD + I], F32, name="t")

        nc.sync.dma_start(out=raw[0][:], in_=query.rearrange("(p j) q -> p j q", j=PACK))
        nc.sync.dma_start(out=words[:].bitcast(I32), in_=keys_words[0].bitcast(I32))
        for quad in range(4):
            nc.scalar.dma_start(
                out=kscale[32 * quad : 32 * quad + 4, :].bitcast(I32),
                in_=keys_scales[0, 4 * quad : 4 * quad + 4, :].bitcast(I32),
            )
        nc.sync.dma_start(out=raw[1][:], in_=query2.rearrange("(p j) q -> p j q", j=PACK))
        nc.sync.dma_start(list1[:], offs)
        nc.sync.dma_start(list2[:], offs2)
        nc.sync.dma_start(out=smear_c[:], in_=smear)
        nc.sync.dma_start(out=lam_c[:], in_=lam)
        nc.sync.dma_start(out=fade_c[:], in_=fade)
        nc.sync.dma_start(out=old_t[:], in_=old)
        nc.vector.memset(half[:], 0.5)
        warm = sb.tile([P, 1], F32, name="warm")
        nc.scalar.activation(warm[:], half[:], ACT.Abs_reciprocal_sqrt, bias=half[:])
        nc.vector.memset(placed[:], 0.0)
        nc.vector.memset(p[:, 0:PAD], 0.0)
        nc.vector.memset(t[:, 0:PAD], 0.0)

        planes = []
        for j in range(2):
            grouped = sb.tile([P, Q, PACK], BF16, name=f"grouped{j}", align_bytes=64)
            codes = sb.tile([P, Q], U32, name=f"codes{j}", align_bytes=64)
            qscale = sb.tile([P, Q], U8, name=f"qscale{j}", align_bytes=64)
            nc.vector.tensor_copy(out=grouped[:], in_=raw[j][:].rearrange("p j q -> p q j"))
            nc.vector.quantize_mx(
                out=codes[:].bitcast(FP8X4), scales=qscale[:], in_=grouped[:].rearrange("p q j -> p (q j)")
            )
            plane = sb.tile([P, T], F32, name=f"plane{j}", tag=f"plane{j}")
            for h in range(len(EDGES) - 1):
                lo, hi = EDGES[h], EDGES[h + 1]
                bank = (j * (len(EDGES) - 1) + h) % 8
                acc = psum.tile([P, hi - lo], F32, name=f"acc{j}{h}", tag=f"acc0{bank}")
                nc.tensor.matmul_mx(
                    out=acc[:],
                    lhsT=codes[:].bitcast(FP8X4),
                    lhsT_scale=qscale[:],
                    rhs=words[:, 2 * lo : 2 * hi].bitcast(FP4X4),
                    rhs_scale=kscale[:, lo:hi],
                    start=True,
                    stop=True,
                )
                cols = plane[:, lo:hi]
                if j == 0 and h % 2 == 1:
                    nc.vector.tensor_copy(out=cols, in_=acc[:])
                else:
                    nc.scalar.copy(out=cols, in_=acc[:])
            planes.append(plane)
        a, b = planes

        def work(name):
            return sb.tile([P, I], F32, name=name)

        H = I // 2
        halves = [slice(0, H), slice(H, I)]
        g1 = sb.tile([P, 2 * I], F32, name="g1")
        g2 = sb.tile([P, 2 * I], F32, name="g2")
        m = sb.tile([P, 2 * I], F32, name="m")
        a1, b1, a2, b2 = g1[:, 0:I], g1[:, I : 2 * I], g2[:, 0:I], g2[:, I : 2 * I]
        sa1, sb1, sb2 = work("sa1"), work("sb1"), work("sb2")
        den, rs, s = work("den"), work("rs"), work("s")
        nc.vector.tensor_copy(a1, a[:].indirect(list1[:]))
        nc.vector.tensor_copy(a2, a[:].indirect(list2[:]))
        nc.scalar.activation(b1, b[:].indirect(list1[:]), ACT.Copy)
        nc.scalar.activation(b2, b[:].indirect(list2[:]), ACT.Copy)
        nc.scalar.activation(sb1[:], b1, ACT.Square)
        for h in halves:
            nc.scalar.activation(sb2[:, h], b2[:, h], ACT.Square)
        sa2 = work("sa2")
        nc.gpsimd.tensor_tensor(sa1[:], a1, a1, ALU.mult)
        nc.vector.tensor_tensor(sa2[:], a2, a2, ALU.mult)
        nc.vector.tensor_tensor(m[:, 0:I], a1, a2, ALU.mult)
        nc.vector.tensor_tensor(m[:, I : 2 * I], b1, b2, ALU.mult)
        la = work("la")
        for h in halves:
            nc.vector.tensor_tensor(la[:, h], sa1[:, h], sb1[:, h], ALU.add)
        lb = sb1
        for j, h in enumerate(halves):
            nc.vector.tensor_tensor(lb[:, h], sa2[:, h], sb2[:, h], ALU.add)
        for h in halves:
            nc.vector.tensor_tensor(den[:, h], la[:, h], lb[:, h], ALU.mult)
            nc.scalar.activation(rs[:, h], den[:, h], ACT.Abs_reciprocal_sqrt, bias=half[:])
        dot = lb
        for h in halves:
            nc.vector.tensor_tensor(dot[:, h], m[:, h], m[:, I + h.start : I + h.stop], ALU.add)
        for h in halves:
            nc.vector.scalar_tensor_tensor(s[:, h], dot[:, h], lam_c[:], rs[:, h], ALU.mult, ALU.mult)
        negmax = sb.tile([P, 1], F32, name="negmax")
        nc.vector.tensor_reduce(negmax[:], s[:], mybir.AxisListType.X, ALU.max, negate=True)

        total = sb.tile([P, 1], F32, name="total")
        inv = sb.tile([P, 1], F32, name="inv")
        gain = sb.tile([P, 1], F32, name="gain")
        own, behind = work("own"), work("behind")
        nc.scalar.activation(p[:, PAD : PAD + I], s[:], ACT.Exp, bias=negmax[:], accum_out=total[:])
        nc.vector.reciprocal(inv[:], total[:])
        for h in halves:
            lo, hi = PAD + h.start, PAD + h.stop
            nc.vector.scalar_tensor_tensor(t[:, lo:hi], p[:, lo - 1 : hi - 1], smear_c[:], p[:, lo:hi], ALU.mult, ALU.add)
            if h.start == 0:
                nc.vector.tensor_scalar(gain[:], inv[:], 256.0, None, ALU.mult)
        nc.scalar.activation(own[:], p[:, PAD : PAD + I], ACT.Copy, scale=gain[:])
        for h in halves:
            lo, hi = PAD + h.start, PAD + h.stop
            nc.vector.tensor_scalar(behind[:, h], t[:, lo - 1 : hi - 1], gain[:], smear_c[:], ALU.mult, ALU.mult)
        nc.vector.tensor_tensor(placed[:].indirect(list1[:]), own[:], behind[:], ALU.add)

        res = sb.tile([P, T], F32, name="res")
        step = T // 4
        for c in range(4):
            cols = slice(c * step, (c + 1) * step)
            nc.vector.scalar_tensor_tensor(res[:, cols], old_t[:, cols], fade_c[:], placed[:, cols], ALU.mult, ALU.add)
            (nc.sync if c % 2 == 0 else nc.scalar).dma_start(out=out[:, cols], in_=res[:, cols])
